import numpy as np
import ml_dtypes


def mxq(x, axis, fmt="e4m3"):
    dtype, down = {"e4m3": (ml_dtypes.float8_e4m3fn, 7), "e5m2": (ml_dtypes.float8_e5m2, 14)}[fmt]
    v = np.moveaxis(np.asarray(x, np.float32).astype(ml_dtypes.bfloat16).astype(np.float64), axis, -1)
    blocks = v.reshape(v.shape[:-1] + (-1, 32))
    amax = np.abs(blocks).max(-1, keepdims=True)
    byte = np.maximum(np.where(amax > 0, np.frexp(amax)[1] - 1 + 127, 0) - down, 1)
    scale = np.exp2(byte - 127.0)
    codes = (blocks / scale).astype(np.float32).astype(dtype).astype(np.float64)
    return np.moveaxis((codes * scale).reshape(v.shape), -1, axis)


WIDE = False


def mx_kscale(k):
    if not WIDE:
        return np.ones(k)
    levels = np.array([10, -10, 5, -5, 0])
    if k % 512:
        return np.exp2(np.random.permutation(np.resize(levels, k // 32))).repeat(32)
    a = np.empty((k // 512, 16))
    for p in range(k // 512):
        a[p, :8] = np.random.permutation(np.resize(levels, 8))
        for g in range(8):
            far = levels[np.abs(levels - a[p, g]) >= 10]
            a[p, g + 8] = far[np.random.randint(len(far))]
    return np.exp2(a.ravel()).repeat(32)


def f64(x):
    return np.asarray(x).astype(np.float64)


def striped(idx):
    return np.tile(idx.reshape(-1, 16).T, (8, 1)).astype(np.uint16)


def unstriped(offs):
    return offs[:16].T.reshape(-1).astype(np.int64)


def striped8(idx):
    return np.concatenate([x.reshape(-1, 16).T for x in idx]).astype(np.uint16)


def runs(offs, k):
    lists = np.stack([offs[16 * r : 16 * r + 16].T.reshape(-1) for r in range(8)]).astype(np.int64)
    return lists[np.arange(k) % 512 // 64]


def pack_weight(w):
    k, n = w.shape
    w = f64(np.asarray(w, np.float32).astype(ml_dtypes.bfloat16)).reshape(k // 32, 32, n)
    amax = np.abs(w).max(1)
    byte = np.clip(np.where(amax > 0, np.frexp(amax)[1] - 1 + 127 - 7, 1), 1, 254)
    scaled = (w * np.exp2(127.0 - byte)[:, None, :]).reshape(k, n).astype(np.float32)
    words = np.ascontiguousarray(scaled.reshape(k // 512, 128, 4, n).transpose(0, 1, 3, 2)).astype(ml_dtypes.float8_e4m3fn).view(np.uint8)
    return words, np.ascontiguousarray(byte.astype(np.uint8).reshape(k // 512, 16, n))


def unpack_weight(words, scales):
    g, p, n, _ = words.shape
    vals = np.ascontiguousarray(words).view(ml_dtypes.float8_e4m3fn).astype(np.float64) * np.repeat(np.exp2(scales.astype(np.float64) - 127.0), 8, axis=1)[..., None]
    return vals.transpose(0, 1, 3, 2).reshape(g * 512, n)


def sigmoid(v):
    return 1.0 / (1.0 + np.exp(-np.maximum(v, -700.0)))


K, T, S, N, H, W = 512, 2048, 512, 512, 512, 256


def setup_inputs():
    n = np.random.standard_normal
    s = mx_kscale(K)[:, None]
    u = mx_kscale(H)
    packed_xT = pack_weight(n((K, T)) * s)
    perm = np.stack([np.random.permutation(S) for _ in range(8)])
    return {
        "x_words": packed_xT[0],
        "x_scales": packed_xT[1],
        "w1": (n((K, H)) / np.sqrt(K) / s).astype(np.float32),
        "gn": (np.random.uniform(0.5, 1.5, (H, 1)) * u[:, None]).astype(np.float32),
        "w2": (n((H, N)) / np.sqrt(2 * H) / u[:, None]).astype(np.float32),
        "w3": (n((K, N)) / np.sqrt(2 * K) / s).astype(np.float32),
        "offs": striped8(np.random.randint(0, T, (8, S))),
        "n1": striped8(perm[:, :W]),
        "n2": striped8(perm[:, W:]),
        "two": striped(np.random.permutation(T)[:S]),
        "n3": striped(np.random.permutation(S)),
    }


def reference(x_words, x_scales, w1, gn, w2, w3, offs, n1, n2, two, n3):
    xq = unpack_weight(x_words, x_scales)[np.arange(K)[:, None], runs(offs, K)]
    y = mxq(f64(w1), 0, "e4m3").T @ xq
    pb = y[np.arange(H)[:, None], runs(n2, H)]
    pa = y[np.arange(H)[:, None], runs(n1, H)]
    rb = pb * sigmoid(pb - pa)
    ra = pa * sigmoid(pa - pb)
    ds = np.zeros((H, S))
    ds[np.arange(H)[:, None], runs(n1, H)] = ra
    dt = ds.copy()
    dt[np.arange(H)[:, None], runs(n2, H)] = rb
    z = f64(gn) * dt
    x_two = unpack_weight(x_words, x_scales)[:, unstriped(two)]
    h = mxq(f64(w2), 0, "e4m3").T @ mxq(z, 0, "e4m3") + mxq(f64(w3), 0, "e4m3").T @ x_two
    st = h - h[:, unstriped(n3)]
    return st - (0.5 * st[:, unstriped(n3)])

@@ -1,0 +1,302 @@
+from contextlib import ExitStack
+
+import concourse.mybir as mybir
+
+K, T, S, N, H, W = 512, 2048, 512, 512, 512, 256
+FLOPS = 2 * 3 * 512 * 512 * 512
+
+F32 = mybir.dt.float32
+BF16 = mybir.dt.bfloat16
+I32 = mybir.dt.int32
+U32 = mybir.dt.uint32
+U16 = mybir.dt.uint16
+U8 = mybir.dt.uint8
+FP8X4 = mybir.dt.float8_e4m3fn_x4
+COPY = mybir.ActivationFunctionType.Copy
+SIGMOID = mybir.ActivationFunctionType.Sigmoid
+MULT = mybir.AluOpType.mult
+ADD = mybir.AluOpType.add
+SUBTRACT = mybir.AluOpType.subtract
+
+P = 128
+PACK = 4
+HALF = S // 2
+
+
+def tile_picked_hmixdueltwice_none_p_kernel(
+    tc, x_words, x_scales, w1, gn, w2, w3, offs, n1, n2, two, n3, out
+):
+    nc = tc.nc
+    with ExitStack() as ctx:
+        lists = ctx.enter_context(tc.tile_pool(name="lists", bufs=1))
+        keep = ctx.enter_context(tc.tile_pool(name="keep", bufs=1))
+        shared = ctx.enter_context(tc.tile_pool(name="shared", bufs=1))
+        psum = ctx.enter_context(tc.psum_pool(name="psum", bufs=1))
+
+        def load_list(src, name):
+            tile = lists.tile(list(src.shape), U16, name=name)
+            nc.sync.dma_start(tile[:], src)
+            return tile
+
+        def load_weight(src, tag):
+            raw = keep.tile([P, PACK, 512], F32, name="raw", tag=tag, align_bytes=64)
+            nc.sync.dma_start(raw[:], src.rearrange("(p j) c -> p j c", j=PACK))
+            return raw
+
+        def quantize(grouped, name, tag=None):
+            width = grouped.shape[1] // PACK
+            codes = keep.tile([P, width], U32, name=name + "_codes", tag=tag or name + "_codes", align_bytes=64)
+            scales = keep.tile([P, width], U8, name=name + "_scales", align_bytes=64)
+            nc.vector.quantize_mx(out=codes[:].bitcast(FP8X4), scales=scales[:], in_=grouped)
+            return codes, scales
+
+        def matmul(bank, weights, block, codes, scales, start, stop):
+            cols = slice(P * block, P * (block + 1))
+            nc.tensor.matmul_mx(
+                out=bank,
+                lhsT=weights[0][:, cols].bitcast(FP8X4),
+                lhsT_scale=weights[1][:, cols],
+                rhs=codes.bitcast(FP8X4),
+                rhs_scale=scales,
+                start=start,
+                stop=stop,
+            )
+
+        table_scales = keep.tile([P, T], U8, name="table_scales", tag="second", align_bytes=64)
+        nc.sync.dma_start(
+            table_scales[:].bitcast(I32), x_scales[0].bitcast(I32).unsqueeze(1).to_broadcast([16, 8, T // 4])
+        )
+        offs_sb = load_list(offs, "offs_sb")
+        two_sb = load_list(two, "two_sb")
+        n1_sb = load_list(n1, "n1_sb")
+        w1_raw = load_weight(w1, "first")
+        table_words = keep.tile([P, T], I32, name="table_words")
+        nc.sync.dma_start(table_words[:], x_words[0].rearrange("p n t -> p (n t)").bitcast(I32))
+        n2_sb = load_list(n2, "n2_sb")
+        n3_sb = load_list(n3, "n3_sb")
+        gain = keep.tile([P, PACK], F32, name="gain")
+        nc.scalar.dma_start(gain[:], gn.rearrange("(p t) o -> p (t o)", t=PACK))
+
+        def pick_scales(offsets, name):
+            picked = keep.tile([P, S], U8, name=name + "_picked")
+            nc.vector.tensor_copy(picked[:], table_scales[:].indirect(offsets[:]))
+            return picked
+
+        def place_scales(picked, name):
+            placed = keep.tile([P, S], U8, name=name + "_placed", align_bytes=64)
+            nc.vector.memset(placed[:].bitcast(I32), 0)
+            for q in range(4):
+                nc.sync.dma_start(
+                    placed[:].bitcast(I32)[32 * q : 32 * q + 4, :], picked[:].bitcast(I32)[32 * q : 32 * (q + 1) : 8, :]
+                )
+            return placed
+
+        hashed_scales = place_scales(pick_scales(offs_sb, "hashed_scales"), "hashed_scales")
+        plain_picked = pick_scales(two_sb, "plain_scales")
+
+        w1_grouped = keep.tile([P, PACK * 512], BF16, name="w1_grouped", align_bytes=64)
+        dealt_out = w1_grouped[:].rearrange("p (t m j) -> p m t j", t=PACK, j=PACK)
+        dealt_in = w1_raw[:].rearrange("p j (m t) -> p m t j", t=PACK)
+        nc.scalar.copy(dealt_out[:, 0:56], dealt_in[:, 0:56])
+        nc.vector.tensor_copy(dealt_out[:, 56:128], dealt_in[:, 56:128])
+        w1_q = quantize(w1_grouped[:], "w1")
+
+        halves = [slice(0, HALF), slice(HALF, S)]
+        hashed_words = keep.tile([P, S], U32, name="hashed_words", align_bytes=64)
+        first_banks = [psum.tile([P, HALF], F32, name="y_bank0_%d" % half, tag="bank%d" % half) for half in range(2)]
+        y_banks = {t: psum.tile([P, S], F32, name="y_bank%d" % t, tag="bank%d" % (t + 1)) for t in range(1, PACK)}
+        for half in range(2):
+            cols = slice(HALF * half, HALF * (half + 1))
+            nc.vector.tensor_copy(
+                hashed_words[:, cols], table_words[:].bitcast(U32).indirect(offs_sb[:, 16 * half : 16 * (half + 1)])
+            )
+        for half, cols in enumerate(halves):
+            matmul(first_banks[half][:], w1_q, 0, hashed_words[:, cols], hashed_scales[:, cols], True, True)
+        for t in range(1, PACK):
+            matmul(y_banks[t][:], w1_q, t, hashed_words[:], hashed_scales[:], True, True)
+
+        plain_words = keep.tile([P, S], U32, name="plain_words", align_bytes=64)
+        nc.vector.tensor_copy(plain_words[:], table_words[:].bitcast(U32).indirect(two_sb[:]))
+
+        def interleave(copy, grouped, planes, cols):
+            copy(
+                grouped[:].rearrange("p (c i j) -> p c j i", i=4, j=PACK)[:, cols.start // 4 : cols.stop // 4],
+                planes[:].rearrange("p j (c i) -> p c j i", i=4)[:, cols.start // 4 : cols.stop // 4],
+            )
+
+        w2_raw = load_weight(w2, "second")
+        plain_scales = place_scales(plain_picked, "plain_scales")
+        w3_raw = load_weight(w3, "first")
+        w3_grouped = keep.tile([P, PACK * 512], BF16, name="w3_grouped", align_bytes=64)
+
+        z_planes = keep.tile([P, PACK, S], BF16, name="z_planes", align_bytes=64)
+        y, pa, pb, diff, dt = {}, {}, {}, {}, {}
+        whole = slice(0, W)
+
+        def offsets_of(tile, part):
+            return tile[:, part.start // 16 : part.stop // 16]
+
+        def leave_psum(t):
+            if t < 2:
+                y[t] = shared.tile([P, S], F32, name="y%d" % t, offset=3072 + 1024 * t)
+            elif t == 2:
+                y[t] = keep.tile([P, S], F32, name="y2", tag="hashed_words", align_bytes=64)
+            else:
+                y[t] = keep.tile([P, S], F32, name="y3")
+            if t == 0:
+                for half, cols in enumerate(halves):
+                    nc.scalar.copy(y[t][:, cols], first_banks[half][:])
+            else:
+                nc.scalar.copy(y[t][:], y_banks[t][:])
+            pa[t] = keep.tile([P, W], F32, name="pa%d" % t)
+            pb[t] = keep.tile([P, W], F32, name="pb%d" % t)
+            diff[t] = keep.tile([P, W], F32, name="diff%d" % t)
+            dt[t] = keep.tile([P, S], F32, name="dt%d" % t)
+
+        def fetch_pairs(t):
+            nc.scalar.activation(pa[t][:], y[t][:].indirect(n1_sb[:]), COPY)
+            if t == 0:
+                nc.vector.tensor_copy(pb[t][:], y[t][:].indirect(n2_sb[:]))
+            else:
+                nc.scalar.activation(pb[t][:], y[t][:].indirect(n2_sb[:]), COPY)
+            nc.vector.tensor_tensor(diff[t][:], pb[t][:], pa[t][:], SUBTRACT)
+
+        def put(t, values, offsets, sign, part=whole):
+            gate = keep.tile([P, part.stop - part.start], F32, name="gate%d_%d_%d" % (t, sign, part.start))
+            nc.scalar.activation(gate[:], diff[t][:, part], SIGMOID, scale=float(sign))
+            nc.vector.tensor_tensor(dt[t][:].indirect(offsets_of(offsets, part)), values[t][:, part], gate[:], MULT)
+
+        z_grouped = keep.tile([P, PACK * S], BF16, name="z_grouped", align_bytes=64)
+
+        def weave_pair(copy, pair, cols):
+            copy(
+                z_grouped[:].rearrange("p (c w e) -> p w c e", w=2, e=2)[:, pair, cols],
+                z_planes[:, 2 * pair : 2 * pair + 2, cols].rearrange("p e c -> p c e"),
+            )
+
+        def round_plane(t, cols):
+            nc.scalar.activation(z_planes[:, t, cols], dt[t][:, cols], COPY, scale=gain[:, t : t + 1])
+
+        quarters = [slice(P * i, P * (i + 1)) for i in range(4)]
+
+        leave_psum(0)
+        fetch_pairs(0)
+        put(0, pb, n2_sb, 1)
+        w2_grouped = shared.tile([P, PACK * 512], BF16, name="w2_grouped", offset=0, align_bytes=64)
+        interleave(nc.vector.tensor_copy, w2_grouped, w2_raw, halves[0])
+        leave_psum(1)
+        fetch_pairs(1)
+        leave_psum(2)
+        put(0, pa, n1_sb, -1)
+        fetch_pairs(2)
+        put(1, pb, n2_sb, 1)
+        leave_psum(3)
+        put(2, pb, n2_sb, 1)
+        fetch_pairs(3)
+        put(1, pa, n1_sb, -1)
+        round_plane(0, slice(0, S))
+        interleave(nc.scalar.copy, w2_grouped, w2_raw, halves[1])
+        put(3, pb, n2_sb, 1)
+        w2_first = quantize(w2_grouped[:, 0 : PACK * P], "w2_first")
+        put(2, pa, n1_sb, -1)
+        interleave(nc.scalar.copy, w3_grouped, w3_raw, halves[0])
+        round_plane(1, slice(0, S))
+        interleave(nc.scalar.copy, w3_grouped, w3_raw, halves[1])
+        w3_q = quantize(w3_grouped[:], "w3")
+        put(3, pa, n1_sb, -1)
+        weave_pair(nc.scalar.copy, 0, slice(0, S))
+        round_plane(2, slice(0, S))
+        h_banks = [
+            [psum.tile([P, HALF], F32, name="h_bank%d_%d" % (m, half), tag="bank%d" % (2 * m + half)) for half in range(2)]
+            for m in range(PACK)
+        ]
+        for m in range(PACK):
+            for half, cols in enumerate(halves):
+                matmul(h_banks[m][half][:], w3_q, m, plain_words[:, cols], plain_scales[:, cols], True, False)
+
+        z_codes = keep.tile([P, S], U32, name="z_codes", align_bytes=64)
+        z_scales = keep.tile([P, S], U8, name="z_scales", align_bytes=64)
+
+        def quantize_z(half):
+            cols = halves[half]
+            nc.vector.quantize_mx(
+                out=z_codes[:, cols].bitcast(FP8X4),
+                scales=z_scales[:, cols],
+                in_=z_grouped[:, PACK * cols.start : PACK * cols.stop],
+            )
+
+        for cols in (halves[0], quarters[2]):
+            nc.vector.tensor_scalar(z_planes[:, 3, cols], dt[3][:, cols], gain[:, 3:4], None, MULT)
+        round_plane(3, quarters[3])
+        weave_pair(nc.scalar.copy, 1, quarters[3])
+        weave_pair(nc.vector.tensor_copy, 1, halves[0])
+        weave_pair(nc.vector.tensor_copy, 1, quarters[2])
+        quantize_z(0)
+        quantize_z(1)
+        w2_rest = quantize(w2_grouped[:, PACK * P :], "w2_rest", tag="z_planes")
+        for m in range(PACK):
+            for half, cols in enumerate(halves):
+                matmul(h_banks[m][half][:], w2_first if m == 0 else w2_rest, max(m - 1, 0), z_codes[:, cols], z_scales[:, cols], False, True)
+
+        n3_halves = [n3_sb[:, 0:16], n3_sb[:, 16:32]]
+        result = {}
+
+        def store(m, cols):
+            nc.sync.dma_start(out[P * m : P * (m + 1), cols], result[m][:, cols])
+
+        def h_from_psum(m, name, scale):
+            tile = keep.tile([P, S], F32, name="%s%d" % (name, m))
+            for half, cols in enumerate(halves):
+                nc.scalar.activation(tile[:, cols], h_banks[m][half][:], COPY, scale=scale)
+            return tile
+
+        def fused_first(m):
+            half_h = h_from_psum(m, "half_h", 0.5)
+            half_h_again = keep.tile([P, S], F32, name="half_h_again%d" % m)
+            for cols in halves:
+                nc.vector.tensor_copy(half_h_again[:, cols], half_h[:, cols])
+            minus_half_st = keep.tile([P, S], F32, name="minus_half_st%d" % m)
+            for offsets, cols in zip(n3_halves, halves):
+                nc.vector.tensor_tensor(minus_half_st[:, cols], half_h[:].indirect(offsets), half_h_again[:, cols], SUBTRACT)
+            return minus_half_st
+
+        def fused_second(m, minus_half_st):
+            st = keep.tile([P, S], F32, name="st%d" % m)
+            if m == 1:
+                nc.vector.tensor_scalar(st[:], minus_half_st[:], -2.0, None, MULT)
+            else:
+                nc.scalar.activation(st[:], minus_half_st[:], COPY, scale=-2.0)
+            result[m] = keep.tile([P, S], F32, name="result%d" % m, tag="result0" if m == 0 else "h_picked3")
+            for offsets, cols in zip(n3_halves, halves):
+                nc.vector.tensor_tensor(result[m][:, cols], minus_half_st[:].indirect(offsets), st[:, cols], ADD)
+                store(m, cols)
+
+        def plain_fetch(window, name):
+            picked = keep.tile([P, S], F32, name=name)
+            for offsets, cols in zip(n3_halves, halves):
+                nc.scalar.activation(picked[:, cols], window[:].indirect(offsets), COPY)
+            return picked
+
+        def plain_first(m, h):
+            picked = plain_fetch(h, "h_picked%d" % m)
+            st = keep.tile([P, S], F32, name="st%d" % m)
+            nc.vector.tensor_tensor(st[:], h[:], picked[:], SUBTRACT)
+            return st
+
+        def plain_second(m, st):
+            picked = plain_fetch(st, "st_picked%d" % m)
+            result[m] = keep.tile([P, S], F32, name="result%d" % m)
+            for cols in halves:
+                nc.vector.scalar_tensor_tensor(result[m][:, cols], picked[:, cols], -0.5, st[:, cols], MULT, ADD)
+                store(m, cols)
+
+        first0 = fused_first(0)
+        first1 = fused_first(1)
+        h2 = h_from_psum(2, "h", 1.0)
+        h3 = h_from_psum(3, "h", 1.0)
+        first2 = plain_first(2, h2)
+        fused_second(0, first0)
+        first3 = plain_first(3, h3)
+        fused_second(1, first1)
+        plain_second(2, first2)
+        plain_second(3, first3)

@@ -77,6 +77,9 @@ def tile_picked_hmixdueltwice_none_p_kernel(
         gain = keep.tile([P, PACK], F32, name="gain")
         nc.scalar.dma_start(gain[:], gn.rearrange("(p t) o -> p (t o)", t=PACK))
 
+        warm = keep.tile([P, 1], F32, name="warm")
+        nc.scalar.activation(warm[:], gain[:, 0:1], SIGMOID)
+
         def pick_scales(offsets, name):
             picked = keep.tile([P, S], U8, name=name + "_picked")
             nc.vector.tensor_copy(picked[:], table_scales[:].indirect(offsets[:]))

@@ -63,22 +63,26 @@ def tile_picked_hmixdueltwice_none_p_kernel(
             )
 
         table_scales = keep.tile([P, T], U8, name="table_scales", tag="second", align_bytes=64)
-        nc.sync.dma_start(
-            table_scales[:].bitcast(I32), x_scales[0].bitcast(I32).unsqueeze(1).to_broadcast([16, 8, T // 4])
-        )
+        nc.vector.memset(table_scales[:].bitcast(I32), 0)
         offs_sb = load_list(offs, "offs_sb")
+        w1_raw = keep.tile([P, PACK, 512], F32, name="raw", tag="first", align_bytes=64)
+        w1_rows = w1.rearrange("(p j) c -> p j c", j=PACK)
+        nc.sync.dma_start(w1_raw[:, 0:1], w1_rows[:, 0:1])
         two_sb = load_list(two, "two_sb")
         n1_sb = load_list(n1, "n1_sb")
-        w1_raw = load_weight(w1, "first")
-        table_words = keep.tile([P, T], I32, name="table_words")
-        nc.sync.dma_start(table_words[:], x_words[0].rearrange("p n t -> p (n t)").bitcast(I32))
         n2_sb = load_list(n2, "n2_sb")
         n3_sb = load_list(n3, "n3_sb")
+        nc.sync.dma_start(table_scales[:].bitcast(I32)[0:P:8, :], x_scales[0].bitcast(I32))
+        nc.sync.dma_start(w1_raw[:, 1:PACK], w1_rows[:, 1:PACK])
+        table_words = keep.tile([P, T], I32, name="table_words")
+        nc.sync.dma_start(table_words[:], x_words[0].rearrange("p n t -> p (n t)").bitcast(I32))
         gain = keep.tile([P, PACK], F32, name="gain")
-        nc.scalar.dma_start(gain[:], gn.rearrange("(p t) o -> p (t o)", t=PACK))
+        nc.sync.dma_start(gain[:], gn.rearrange("(p t) o -> p (t o)", t=PACK))
 
+        warm_in = keep.tile([P, 1], F32, name="warm_in")
+        nc.vector.memset(warm_in[:], 0.0)
         warm = keep.tile([P, 1], F32, name="warm")
-        nc.scalar.activation(warm[:], gain[:, 0:1], SIGMOID)
+        nc.scalar.activation(warm[:], warm_in[:], SIGMOID)
 
         def pick_scales(offsets, name):
             picked = keep.tile([P, S], U8, name=name + "_picked")
@@ -100,22 +104,23 @@ def tile_picked_hmixdueltwice_none_p_kernel(
         w1_grouped = keep.tile([P, PACK * 512], BF16, name="w1_grouped", align_bytes=64)
         dealt_out = w1_grouped[:].rearrange("p (t m j) -> p m t j", t=PACK, j=PACK)
         dealt_in = w1_raw[:].rearrange("p j (m t) -> p m t j", t=PACK)
-        nc.scalar.copy(dealt_out[:, 0:56], dealt_in[:, 0:56])
-        nc.vector.tensor_copy(dealt_out[:, 56:128], dealt_in[:, 56:128])
+        nc.scalar.copy(dealt_out[:, 0:64], dealt_in[:, 0:64])
+        nc.vector.tensor_copy(dealt_out[:, 64:128], dealt_in[:, 64:128])
         w1_q = quantize(w1_grouped[:], "w1")
 
         halves = [slice(0, HALF), slice(HALF, S)]
         hashed_words = keep.tile([P, S], U32, name="hashed_words", align_bytes=64)
         first_banks = [psum.tile([P, HALF], F32, name="y_bank0_%d" % half, tag="bank%d" % half) for half in range(2)]
-        y_banks = {t: psum.tile([P, S], F32, name="y_bank%d" % t, tag="bank%d" % (t + 1)) for t in range(1, PACK)}
+        turn = [1, 3, 0, 2]
+        y_banks = {t: psum.tile([P, S], F32, name="y_bank%d" % t, tag="bank%d" % (i + 2)) for i, t in enumerate(turn[1:])}
         for half in range(2):
             cols = slice(HALF * half, HALF * (half + 1))
             nc.vector.tensor_copy(
                 hashed_words[:, cols], table_words[:].bitcast(U32).indirect(offs_sb[:, 16 * half : 16 * (half + 1)])
             )
         for half, cols in enumerate(halves):
-            matmul(first_banks[half][:], w1_q, 0, hashed_words[:, cols], hashed_scales[:, cols], True, True)
-        for t in range(1, PACK):
+            matmul(first_banks[half][:], w1_q, turn[0], hashed_words[:, cols], hashed_scales[:, cols], True, True)
+        for t in turn[1:]:
             matmul(y_banks[t][:], w1_q, t, hashed_words[:], hashed_scales[:], True, True)
 
         plain_words = keep.tile([P, S], U32, name="plain_words", align_bytes=64)
@@ -132,21 +137,20 @@ def tile_picked_hmixdueltwice_none_p_kernel(
         w3_raw = load_weight(w3, "first")
         w3_grouped = keep.tile([P, PACK * 512], BF16, name="w3_grouped", align_bytes=64)
 
-        z_planes = keep.tile([P, PACK, S], BF16, name="z_planes", align_bytes=64)
         y, pa, pb, diff, dt = {}, {}, {}, {}, {}
-        whole = slice(0, W)
+        gate = {}
 
         def offsets_of(tile, part):
             return tile[:, part.start // 16 : part.stop // 16]
 
         def leave_psum(t):
-            if t < 2:
-                y[t] = shared.tile([P, S], F32, name="y%d" % t, offset=3072 + 1024 * t)
-            elif t == 2:
-                y[t] = keep.tile([P, S], F32, name="y2", tag="hashed_words", align_bytes=64)
+            if t in turn[:2]:
+                y[t] = shared.tile([P, S], F32, name="y%d" % t, offset=3072 + 1024 * turn.index(t))
+            elif t == turn[2]:
+                y[t] = keep.tile([P, S], F32, name="y%d" % t, tag="hashed_words", align_bytes=64)
             else:
-                y[t] = keep.tile([P, S], F32, name="y3")
-            if t == 0:
+                y[t] = keep.tile([P, S], F32, name="y%d" % t)
+            if t == turn[0]:
                 for half, cols in enumerate(halves):
                     nc.scalar.copy(y[t][:, cols], first_banks[half][:])
             else:
@@ -154,61 +158,81 @@ def tile_picked_hmixdueltwice_none_p_kernel(
             pa[t] = keep.tile([P, W], F32, name="pa%d" % t)
             pb[t] = keep.tile([P, W], F32, name="pb%d" % t)
             diff[t] = keep.tile([P, W], F32, name="diff%d" % t)
-            dt[t] = keep.tile([P, S], F32, name="dt%d" % t)
+            dt[t] = keep.tile([P, S if t % 2 else 2 * S], F32, name="dt%d" % t, align_bytes=64)
 
         def fetch_pairs(t):
             nc.scalar.activation(pa[t][:], y[t][:].indirect(n1_sb[:]), COPY)
-            if t == 0:
+            if t == turn[0]:
                 nc.vector.tensor_copy(pb[t][:], y[t][:].indirect(n2_sb[:]))
             else:
                 nc.scalar.activation(pb[t][:], y[t][:].indirect(n2_sb[:]), COPY)
             nc.vector.tensor_tensor(diff[t][:], pb[t][:], pa[t][:], SUBTRACT)
 
-        def put(t, values, offsets, sign, part=whole):
-            gate = keep.tile([P, part.stop - part.start], F32, name="gate%d_%d_%d" % (t, sign, part.start))
-            nc.scalar.activation(gate[:], diff[t][:, part], SIGMOID, scale=float(sign))
-            nc.vector.tensor_tensor(dt[t][:].indirect(offsets_of(offsets, part)), values[t][:, part], gate[:], MULT)
+        def make_gate(t, sign):
+            gate[t, sign] = keep.tile([P, W], F32, name="gate%d_%d" % (t, sign))
+            nc.scalar.activation(gate[t, sign][:], diff[t][:], SIGMOID, scale=float(sign))
+
+        def gain_gate(t, sign):
+            plain = gate[t, sign]
+            gate[t, sign] = keep.tile([P, W], F32, name="gained%d_%d" % (t, sign))
+            nc.scalar.activation(gate[t, sign][:], plain[:], COPY, scale=gain[:, t : t + 1])
+
+        def put(t, sign):
+            values, offsets = (pb, n2_sb) if sign > 0 else (pa, n1_sb)
+            nc.vector.tensor_tensor(dt[t][:].indirect(offsets[:]), values[t][:], gate[t, sign][:], MULT)
+
+        def join(t):
+            nc.scalar.activation(dt[t - 1][:, S:], dt[t][:], COPY, scale=gain[:, t : t + 1])
 
         z_grouped = keep.tile([P, PACK * S], BF16, name="z_grouped", align_bytes=64)
 
         def weave_pair(copy, pair, cols):
             copy(
                 z_grouped[:].rearrange("p (c w e) -> p w c e", w=2, e=2)[:, pair, cols],
-                z_planes[:, 2 * pair : 2 * pair + 2, cols].rearrange("p e c -> p c e"),
+                dt[2 * pair][:].rearrange("p (e c) -> p c e", e=2)[:, cols],
             )
 
-        def round_plane(t, cols):
-            nc.scalar.activation(z_planes[:, t, cols], dt[t][:, cols], COPY, scale=gain[:, t : t + 1])
-
         quarters = [slice(P * i, P * (i + 1)) for i in range(4)]
+        every = slice(0, S)
 
-        leave_psum(0)
-        fetch_pairs(0)
-        put(0, pb, n2_sb, 1)
-        w2_grouped = shared.tile([P, PACK * 512], BF16, name="w2_grouped", offset=0, align_bytes=64)
-        interleave(nc.vector.tensor_copy, w2_grouped, w2_raw, halves[0])
         leave_psum(1)
         fetch_pairs(1)
-        leave_psum(2)
-        put(0, pa, n1_sb, -1)
-        fetch_pairs(2)
-        put(1, pb, n2_sb, 1)
+        make_gate(1, 1)
+        put(1, 1)
+        w2_grouped = shared.tile([P, PACK * 512], BF16, name="w2_grouped", offset=0, align_bytes=64)
+        interleave(nc.vector.tensor_copy, w2_grouped, w2_raw, halves[0])
         leave_psum(3)
-        put(2, pb, n2_sb, 1)
         fetch_pairs(3)
-        put(1, pa, n1_sb, -1)
-        round_plane(0, slice(0, S))
-        interleave(nc.scalar.copy, w2_grouped, w2_raw, halves[1])
-        put(3, pb, n2_sb, 1)
+        leave_psum(0)
+        make_gate(1, -1)
+        put(1, -1)
+        fetch_pairs(0)
+        make_gate(3, 1)
+        put(3, 1)
+        leave_psum(2)
+        make_gate(0, 1)
+        join(1)
+        gain_gate(0, 1)
+        put(0, 1)
+        fetch_pairs(2)
+        make_gate(0, -1)
+        make_gate(3, -1)
+        put(3, -1)
         w2_first = quantize(w2_grouped[:, 0 : PACK * P], "w2_first")
-        put(2, pa, n1_sb, -1)
+        gain_gate(0, -1)
+        put(0, -1)
         interleave(nc.scalar.copy, w3_grouped, w3_raw, halves[0])
-        round_plane(1, slice(0, S))
+        make_gate(2, 1)
+        make_gate(2, -1)
+        gain_gate(2, 1)
+        join(3)
+        put(2, 1)
         interleave(nc.scalar.copy, w3_grouped, w3_raw, halves[1])
         w3_q = quantize(w3_grouped[:], "w3")
-        put(3, pa, n1_sb, -1)
-        weave_pair(nc.scalar.copy, 0, slice(0, S))
-        round_plane(2, slice(0, S))
+        gain_gate(2, -1)
+        put(2, -1)
+        weave_pair(nc.scalar.copy, 0, every)
+        interleave(nc.scalar.copy, w2_grouped, w2_raw, halves[1])
         h_banks = [
             [psum.tile([P, HALF], F32, name="h_bank%d_%d" % (m, half), tag="bank%d" % (2 * m + half)) for half in range(2)]
             for m in range(PACK)
@@ -228,15 +252,12 @@ def tile_picked_hmixdueltwice_none_p_kernel(
                 in_=z_grouped[:, PACK * cols.start : PACK * cols.stop],
             )
 
-        for cols in (halves[0], quarters[2]):
-            nc.vector.tensor_scalar(z_planes[:, 3, cols], dt[3][:, cols], gain[:, 3:4], None, MULT)
-        round_plane(3, quarters[3])
-        weave_pair(nc.scalar.copy, 1, quarters[3])
         weave_pair(nc.vector.tensor_copy, 1, halves[0])
+        weave_pair(nc.scalar.copy, 1, quarters[3])
         weave_pair(nc.vector.tensor_copy, 1, quarters[2])
         quantize_z(0)
         quantize_z(1)
-        w2_rest = quantize(w2_grouped[:, PACK * P :], "w2_rest", tag="z_planes")
+        w2_rest = quantize(w2_grouped[:, PACK * P :], "w2_rest", tag="dt2")
         for m in range(PACK):
             for half, cols in enumerate(halves):
                 matmul(h_banks[m][half][:], w2_first if m == 0 else w2_rest, max(m - 1, 0), z_codes[:, cols], z_scales[:, cols], False, True)
@@ -265,19 +286,19 @@ def tile_picked_hmixdueltwice_none_p_kernel(
 
         def fused_second(m, minus_half_st):
             st = keep.tile([P, S], F32, name="st%d" % m)
-            if m == 1:
+            if m == 5:
                 nc.vector.tensor_scalar(st[:], minus_half_st[:], -2.0, None, MULT)
             else:
                 nc.scalar.activation(st[:], minus_half_st[:], COPY, scale=-2.0)
-            result[m] = keep.tile([P, S], F32, name="result%d" % m, tag="result0" if m == 0 else "h_picked3")
+            result[m] = keep.tile([P, S], F32, name="result%d" % m)
             for offsets, cols in zip(n3_halves, halves):
                 nc.vector.tensor_tensor(result[m][:, cols], minus_half_st[:].indirect(offsets), st[:, cols], ADD)
                 store(m, cols)
 
-        def plain_fetch(window, name):
+        def plain_fetch(window, name, pieces=halves):
             picked = keep.tile([P, S], F32, name=name)
-            for offsets, cols in zip(n3_halves, halves):
-                nc.scalar.activation(picked[:, cols], window[:].indirect(offsets), COPY)
+            for cols in pieces:
+                nc.scalar.activation(picked[:, cols], window[:].indirect(offsets_of(n3_sb, cols)), COPY)
             return picked
 
         def plain_first(m, h):
@@ -286,10 +307,10 @@ def tile_picked_hmixdueltwice_none_p_kernel(
             nc.vector.tensor_tensor(st[:], h[:], picked[:], SUBTRACT)
             return st
 
-        def plain_second(m, st):
-            picked = plain_fetch(st, "st_picked%d" % m)
+        def plain_second(m, st, pieces):
+            picked = plain_fetch(st, "st_picked%d" % m, pieces)
             result[m] = keep.tile([P, S], F32, name="result%d" % m)
-            for cols in halves:
+            for cols in pieces:
                 nc.vector.scalar_tensor_tensor(result[m][:, cols], picked[:, cols], -0.5, st[:, cols], MULT, ADD)
                 store(m, cols)
 
@@ -301,5 +322,5 @@ def tile_picked_hmixdueltwice_none_p_kernel(
         fused_second(0, first0)
         first3 = plain_first(3, h3)
         fused_second(1, first1)
-        plain_second(2, first2)
-        plain_second(3, first3)
+        plain_second(2, first2, halves)
+        plain_second(3, first3, [halves[0], quarters[2], quarters[3]])

from contextlib import ExitStack

import concourse.mybir as mybir

K, T, S, N, H, W = 512, 2048, 512, 512, 512, 256
FLOPS = 2 * 3 * 512 * 512 * 512

F32 = mybir.dt.float32
BF16 = mybir.dt.bfloat16
I32 = mybir.dt.int32
U32 = mybir.dt.uint32
U16 = mybir.dt.uint16
U8 = mybir.dt.uint8
FP8X4 = mybir.dt.float8_e4m3fn_x4
COPY = mybir.ActivationFunctionType.Copy
SIGMOID = mybir.ActivationFunctionType.Sigmoid
MULT = mybir.AluOpType.mult
ADD = mybir.AluOpType.add
SUBTRACT = mybir.AluOpType.subtract

P = 128
PACK = 4
HALF = S // 2


def tile_picked_hmixdueltwice_none_p_kernel(
    tc, x_words, x_scales, w1, gn, w2, w3, offs, n1, n2, two, n3, out
):
    nc = tc.nc
    with ExitStack() as ctx:
        lists = ctx.enter_context(tc.tile_pool(name="lists", bufs=1))
        keep = ctx.enter_context(tc.tile_pool(name="keep", bufs=1))
        shared = ctx.enter_context(tc.tile_pool(name="shared", bufs=1))
        psum = ctx.enter_context(tc.psum_pool(name="psum", bufs=1))

        def load_list(src, name):
            tile = lists.tile(list(src.shape), U16, name=name)
            nc.sync.dma_start(tile[:], src)
            return tile

        def load_weight(src, tag):
            raw = keep.tile([P, PACK, 512], F32, name="raw", tag=tag, align_bytes=64)
            nc.sync.dma_start(raw[:], src.rearrange("(p j) c -> p j c", j=PACK))
            return raw

        def quantize(grouped, name, tag=None):
            width = grouped.shape[1] // PACK
            codes = keep.tile([P, width], U32, name=name + "_codes", tag=tag or name + "_codes", align_bytes=64)
            scales = keep.tile([P, width], U8, name=name + "_scales", align_bytes=64)
            nc.vector.quantize_mx(out=codes[:].bitcast(FP8X4), scales=scales[:], in_=grouped)
            return codes, scales

        def matmul(bank, weights, block, codes, scales, start, stop):
            cols = slice(P * block, P * (block + 1))
            nc.tensor.matmul_mx(
                out=bank,
                lhsT=weights[0][:, cols].bitcast(FP8X4),
                lhsT_scale=weights[1][:, cols],
                rhs=codes.bitcast(FP8X4),
                rhs_scale=scales,
                start=start,
                stop=stop,
            )

        table_scales = keep.tile([P, T], U8, name="table_scales", tag="second", align_bytes=64)
        nc.vector.memset(table_scales[:].bitcast(I32), 0)
        offs_sb = load_list(offs, "offs_sb")
        w1_raw = keep.tile([P, PACK, 512], F32, name="raw", tag="first", align_bytes=64)
        w1_rows = w1.rearrange("(p j) c -> p j c", j=PACK)
        nc.sync.dma_start(w1_raw[:, 0:1], w1_rows[:, 0:1])
        two_sb = load_list(two, "two_sb")
        n1_sb = load_list(n1, "n1_sb")
        n2_sb = load_list(n2, "n2_sb")
        n3_sb = load_list(n3, "n3_sb")
        nc.sync.dma_start(table_scales[:].bitcast(I32)[0:P:8, :], x_scales[0].bitcast(I32))
        nc.sync.dma_start(w1_raw[:, 1:PACK], w1_rows[:, 1:PACK])
        table_words = keep.tile([P, T], I32, name="table_words")
        nc.sync.dma_start(table_words[:], x_words[0].rearrange("p n t -> p (n t)").bitcast(I32))
        gain = keep.tile([P, PACK], F32, name="gain")
        nc.sync.dma_start(gain[:], gn.rearrange("(p t) o -> p (t o)", t=PACK))

        warm_in = keep.tile([P, 1], F32, name="warm_in")
        nc.vector.memset(warm_in[:], 0.0)
        warm = keep.tile([P, 1], F32, name="warm")
        nc.scalar.activation(warm[:], warm_in[:], SIGMOID)

        def pick_scales(offsets, name):
            picked = keep.tile([P, S], U8, name=name + "_picked")
            nc.vector.tensor_copy(picked[:], table_scales[:].indirect(offsets[:]))
            return picked

        def place_scales(picked, name):
            placed = keep.tile([P, S], U8, name=name + "_placed", align_bytes=64)
            nc.vector.memset(placed[:].bitcast(I32), 0)
            for q in range(4):
                nc.sync.dma_start(
                    placed[:].bitcast(I32)[32 * q : 32 * q + 4, :], picked[:].bitcast(I32)[32 * q : 32 * (q + 1) : 8, :]
                )
            return placed

        hashed_scales = place_scales(pick_scales(offs_sb, "hashed_scales"), "hashed_scales")
        plain_picked = pick_scales(two_sb, "plain_scales")

        w1_grouped = keep.tile([P, PACK * 512], BF16, name="w1_grouped", align_bytes=64)
        dealt_out = w1_grouped[:].rearrange("p (t m j) -> p m t j", t=PACK, j=PACK)
        dealt_in = w1_raw[:].rearrange("p j (m t) -> p m t j", t=PACK)
        nc.scalar.copy(dealt_out[:, 0:64], dealt_in[:, 0:64])
        nc.vector.tensor_copy(dealt_out[:, 64:128], dealt_in[:, 64:128])
        w1_q = quantize(w1_grouped[:], "w1")

        halves = [slice(0, HALF), slice(HALF, S)]
        hashed_words = keep.tile([P, S], U32, name="hashed_words", align_bytes=64)
        first_banks = [psum.tile([P, HALF], F32, name="y_bank0_%d" % half, tag="bank%d" % half) for half in range(2)]
        turn = [1, 3, 0, 2]
        y_banks = {t: psum.tile([P, S], F32, name="y_bank%d" % t, tag="bank%d" % (i + 2)) for i, t in enumerate(turn[1:])}
        for half in range(2):
            cols = slice(HALF * half, HALF * (half + 1))
            nc.vector.tensor_copy(
                hashed_words[:, cols], table_words[:].bitcast(U32).indirect(offs_sb[:, 16 * half : 16 * (half + 1)])
            )
        for half, cols in enumerate(halves):
            matmul(first_banks[half][:], w1_q, turn[0], hashed_words[:, cols], hashed_scales[:, cols], True, True)
        for t in turn[1:]:
            matmul(y_banks[t][:], w1_q, t, hashed_words[:], hashed_scales[:], True, True)

        plain_words = keep.tile([P, S], U32, name="plain_words", align_bytes=64)
        nc.vector.tensor_copy(plain_words[:], table_words[:].bitcast(U32).indirect(two_sb[:]))

        def interleave(copy, grouped, planes, cols):
            copy(
                grouped[:].rearrange("p (c i j) -> p c j i", i=4, j=PACK)[:, cols.start // 4 : cols.stop // 4],
                planes[:].rearrange("p j (c i) -> p c j i", i=4)[:, cols.start // 4 : cols.stop // 4],
            )

        w2_raw = load_weight(w2, "second")
        plain_scales = place_scales(plain_picked, "plain_scales")
        w3_raw = load_weight(w3, "first")
        w3_grouped = keep.tile([P, PACK * 512], BF16, name="w3_grouped", align_bytes=64)

        y, pa, pb, diff, dt = {}, {}, {}, {}, {}
        gate = {}

        def offsets_of(tile, part):
            return tile[:, part.start // 16 : part.stop // 16]

        def leave_psum(t):
            if t in turn[:2]:
                y[t] = shared.tile([P, S], F32, name="y%d" % t, offset=3072 + 1024 * turn.index(t))
            elif t == turn[2]:
                y[t] = keep.tile([P, S], F32, name="y%d" % t, tag="hashed_words", align_bytes=64)
            else:
                y[t] = keep.tile([P, S], F32, name="y%d" % t)
            if t == turn[0]:
                for half, cols in enumerate(halves):
                    nc.scalar.copy(y[t][:, cols], first_banks[half][:])
            else:
                nc.scalar.copy(y[t][:], y_banks[t][:])
            pa[t] = keep.tile([P, W], F32, name="pa%d" % t)
            pb[t] = keep.tile([P, W], F32, name="pb%d" % t)
            diff[t] = keep.tile([P, W], F32, name="diff%d" % t)
            dt[t] = keep.tile([P, S if t % 2 else 2 * S], F32, name="dt%d" % t, align_bytes=64)

        def fetch_pairs(t):
            nc.scalar.activation(pa[t][:], y[t][:].indirect(n1_sb[:]), COPY)
            if t == turn[0]:
                nc.vector.tensor_copy(pb[t][:], y[t][:].indirect(n2_sb[:]))
            else:
                nc.scalar.activation(pb[t][:], y[t][:].indirect(n2_sb[:]), COPY)
            nc.vector.tensor_tensor(diff[t][:], pb[t][:], pa[t][:], SUBTRACT)

        def make_gate(t, sign):
            gate[t, sign] = keep.tile([P, W], F32, name="gate%d_%d" % (t, sign))
            nc.scalar.activation(gate[t, sign][:], diff[t][:], SIGMOID, scale=float(sign))

        def gain_gate(t, sign):
            plain = gate[t, sign]
            gate[t, sign] = keep.tile([P, W], F32, name="gained%d_%d" % (t, sign))
            nc.scalar.activation(gate[t, sign][:], plain[:], COPY, scale=gain[:, t : t + 1])

        def put(t, sign):
            values, offsets = (pb, n2_sb) if sign > 0 else (pa, n1_sb)
            nc.vector.tensor_tensor(dt[t][:].indirect(offsets[:]), values[t][:], gate[t, sign][:], MULT)

        def join(t):
            nc.scalar.activation(dt[t - 1][:, S:], dt[t][:], COPY, scale=gain[:, t : t + 1])

        z_grouped = keep.tile([P, PACK * S], BF16, name="z_grouped", align_bytes=64)

        def weave_pair(copy, pair, cols):
            copy(
                z_grouped[:].rearrange("p (c w e) -> p w c e", w=2, e=2)[:, pair, cols],
                dt[2 * pair][:].rearrange("p (e c) -> p c e", e=2)[:, cols],
            )

        quarters = [slice(P * i, P * (i + 1)) for i in range(4)]
        every = slice(0, S)

        leave_psum(1)
        fetch_pairs(1)
        make_gate(1, 1)
        put(1, 1)
        w2_grouped = shared.tile([P, PACK * 512], BF16, name="w2_grouped", offset=0, align_bytes=64)
        interleave(nc.vector.tensor_copy, w2_grouped, w2_raw, halves[0])
        leave_psum(3)
        fetch_pairs(3)
        leave_psum(0)
        make_gate(1, -1)
        put(1, -1)
        fetch_pairs(0)
        make_gate(3, 1)
        put(3, 1)
        leave_psum(2)
        make_gate(0, 1)
        join(1)
        gain_gate(0, 1)
        put(0, 1)
        fetch_pairs(2)
        make_gate(0, -1)
        make_gate(3, -1)
        put(3, -1)
        w2_first = quantize(w2_grouped[:, 0 : PACK * P], "w2_first")
        gain_gate(0, -1)
        put(0, -1)
        interleave(nc.scalar.copy, w3_grouped, w3_raw, halves[0])
        make_gate(2, 1)
        make_gate(2, -1)
        gain_gate(2, 1)
        join(3)
        put(2, 1)
        interleave(nc.scalar.copy, w3_grouped, w3_raw, halves[1])
        w3_q = quantize(w3_grouped[:], "w3")
        gain_gate(2, -1)
        put(2, -1)
        weave_pair(nc.scalar.copy, 0, every)
        interleave(nc.scalar.copy, w2_grouped, w2_raw, halves[1])
        h_banks = [
            [psum.tile([P, HALF], F32, name="h_bank%d_%d" % (m, half), tag="bank%d" % (2 * m + half)) for half in range(2)]
            for m in range(PACK)
        ]
        for m in range(PACK):
            for half, cols in enumerate(halves):
                matmul(h_banks[m][half][:], w3_q, m, plain_words[:, cols], plain_scales[:, cols], True, False)

        z_codes = keep.tile([P, S], U32, name="z_codes", align_bytes=64)
        z_scales = keep.tile([P, S], U8, name="z_scales", align_bytes=64)

        def quantize_z(half):
            cols = halves[half]
            nc.vector.quantize_mx(
                out=z_codes[:, cols].bitcast(FP8X4),
                scales=z_scales[:, cols],
                in_=z_grouped[:, PACK * cols.start : PACK * cols.stop],
            )

        weave_pair(nc.vector.tensor_copy, 1, halves[0])
        weave_pair(nc.scalar.copy, 1, quarters[3])
        weave_pair(nc.vector.tensor_copy, 1, quarters[2])
        quantize_z(0)
        quantize_z(1)
        w2_rest = quantize(w2_grouped[:, PACK * P :], "w2_rest", tag="dt2")
        for m in range(PACK):
            for half, cols in enumerate(halves):
                matmul(h_banks[m][half][:], w2_first if m == 0 else w2_rest, max(m - 1, 0), z_codes[:, cols], z_scales[:, cols], False, True)

        n3_halves = [n3_sb[:, 0:16], n3_sb[:, 16:32]]
        result = {}

        def store(m, cols):
            nc.sync.dma_start(out[P * m : P * (m + 1), cols], result[m][:, cols])

        def h_from_psum(m, name, scale):
            tile = keep.tile([P, S], F32, name="%s%d" % (name, m))
            for half, cols in enumerate(halves):
                nc.scalar.activation(tile[:, cols], h_banks[m][half][:], COPY, scale=scale)
            return tile

        def fused_first(m):
            half_h = h_from_psum(m, "half_h", 0.5)
            half_h_again = keep.tile([P, S], F32, name="half_h_again%d" % m)
            for cols in halves:
                nc.vector.tensor_copy(half_h_again[:, cols], half_h[:, cols])
            minus_half_st = keep.tile([P, S], F32, name="minus_half_st%d" % m)
            for offsets, cols in zip(n3_halves, halves):
                nc.vector.tensor_tensor(minus_half_st[:, cols], half_h[:].indirect(offsets), half_h_again[:, cols], SUBTRACT)
            return minus_half_st

        def fused_second(m, minus_half_st):
            st = keep.tile([P, S], F32, name="st%d" % m)
            if m == 5:
                nc.vector.tensor_scalar(st[:], minus_half_st[:], -2.0, None, MULT)
            else:
                nc.scalar.activation(st[:], minus_half_st[:], COPY, scale=-2.0)
            result[m] = keep.tile([P, S], F32, name="result%d" % m)
            for offsets, cols in zip(n3_halves, halves):
                nc.vector.tensor_tensor(result[m][:, cols], minus_half_st[:].indirect(offsets), st[:, cols], ADD)
                store(m, cols)

        def plain_fetch(window, name, pieces=halves):
            picked = keep.tile([P, S], F32, name=name)
            for cols in pieces:
                nc.scalar.activation(picked[:, cols], window[:].indirect(offsets_of(n3_sb, cols)), COPY)
            return picked

        def plain_first(m, h):
            picked = plain_fetch(h, "h_picked%d" % m)
            st = keep.tile([P, S], F32, name="st%d" % m)
            nc.vector.tensor_tensor(st[:], h[:], picked[:], SUBTRACT)
            return st

        def plain_second(m, st, pieces):
            picked = plain_fetch(st, "st_picked%d" % m, pieces)
            result[m] = keep.tile([P, S], F32, name="result%d" % m)
            for cols in pieces:
                nc.vector.scalar_tensor_tensor(result[m][:, cols], picked[:, cols], -0.5, st[:, cols], MULT, ADD)
                store(m, cols)

        first0 = fused_first(0)
        first1 = fused_first(1)
        h2 = h_from_psum(2, "h", 1.0)
        h3 = h_from_psum(3, "h", 1.0)
        first2 = plain_first(2, h2)
        fused_second(0, first0)
        first3 = plain_first(3, h3)
        fused_second(1, first1)
        plain_second(2, first2, halves)
        plain_second(3, first3, [halves[0], quarters[2], quarters[3]])
